import numpy as np
import ml_dtypes


def mxq(x, axis, fmt="e4m3"):
    dtype, down = {"e4m3": (ml_dtypes.float8_e4m3fn, 7), "e5m2": (ml_dtypes.float8_e5m2, 14)}[fmt]
    v = np.moveaxis(np.asarray(x, np.float32).astype(ml_dtypes.bfloat16).astype(np.float64), axis, -1)
    blocks = v.reshape(v.shape[:-1] + (-1, 32))
    amax = np.abs(blocks).max(-1, keepdims=True)
    byte = np.maximum(np.where(amax > 0, np.frexp(amax)[1] - 1 + 127, 0) - down, 1)
    scale = np.exp2(byte - 127.0)
    codes = (blocks / scale).astype(np.float32).astype(dtype).astype(np.float64)
    return np.moveaxis((codes * scale).reshape(v.shape), -1, axis)


WIDE = False


def mx_kscale(k):
    if not WIDE:
        return np.ones(k)
    levels = np.array([10, -10, 5, -5, 0])
    if k % 512:
        return np.exp2(np.random.permutation(np.resize(levels, k // 32))).repeat(32)
    a = np.empty((k // 512, 16))
    for p in range(k // 512):
        a[p, :8] = np.random.permutation(np.resize(levels, 8))
        for g in range(8):
            far = levels[np.abs(levels - a[p, g]) >= 10]
            a[p, g + 8] = far[np.random.randint(len(far))]
    return np.exp2(a.ravel()).repeat(32)


def f64(x):
    return np.asarray(x).astype(np.float64)


def striped(idx):
    return np.tile(idx.reshape(-1, 16).T, (8, 1)).astype(np.uint16)


def unstriped(offs):
    return offs[:16].T.reshape(-1).astype(np.int64)


def striped8(idx):
    return np.concatenate([x.reshape(-1, 16).T for x in idx]).astype(np.uint16)


def runs(offs, k):
    lists = np.stack([offs[16 * r : 16 * r + 16].T.reshape(-1) for r in range(8)]).astype(np.int64)
    return lists[np.arange(k) % 512 // 64]


def pack_weight(w):
    k, n = w.shape
    w = f64(np.asarray(w, np.float32).astype(ml_dtypes.bfloat16)).reshape(k // 32, 32, n)
    amax = np.abs(w).max(1)
    byte = np.clip(np.where(amax > 0, np.frexp(amax)[1] - 1 + 127 - 7, 1), 1, 254)
    scaled = (w * np.exp2(127.0 - byte)[:, None, :]).reshape(k, n).astype(np.float32)
    words = np.ascontiguousarray(scaled.reshape(k // 512, 128, 4, n).transpose(0, 1, 3, 2)).astype(ml_dtypes.float8_e4m3fn).view(np.uint8)
    return words, np.ascontiguousarray(byte.astype(np.uint8).reshape(k // 512, 16, n))


def unpack_weight(words, scales):
    g, p, n, _ = words.shape
    vals = np.ascontiguousarray(words).view(ml_dtypes.float8_e4m3fn).astype(np.float64) * np.repeat(np.exp2(scales.astype(np.float64) - 127.0), 8, axis=1)[..., None]
    return vals.transpose(0, 1, 3, 2).reshape(g * 512, n)


def sigmoid(v):
    return 1.0 / (1.0 + np.exp(-np.maximum(v, -700.0)))


K, T, S, V, H, C, W = 512, 2048, 1024, 512, 512, 512, 256


def setup_inputs():
    n = np.random.standard_normal
    s = mx_kscale(K)[:, None]
    packed_xT = pack_weight(n((K, T)) * s)
    perm = np.stack([np.random.permutation(V) for _ in range(8)])
    return {
        "x_words": packed_xT[0],
        "x_scales": packed_xT[1],
        "w1": (n((K, H)) / np.sqrt(K) / s).astype(np.float32),
        "gs": (np.random.uniform(0.5, 1.5, (K, 1)) / s).astype(np.float32),
        "offs": striped(np.random.permutation(T)[:S]),
        "n1": striped8(np.stack([np.random.permutation(S) for _ in range(8)])),
        "cand": striped(np.random.permutation(T)[:C]),
        "n2": striped8(perm[:, :W]),
        "n3": striped8(perm[:, W:]),
    }


def reference(x_words, x_scales, w1, gs, offs, n1, cand, n2, n3):
    x_cand = unpack_weight(x_words, x_scales)[:, unstriped(cand)]
    xq = unpack_weight(x_words, x_scales)[:, unstriped(offs)]
    y = mxq(f64(w1), 0, "e4m3").T @ xq
    ln = y[np.arange(H)[:, None], runs(n1, H)]
    mx = ln.reshape(H, V, 2).max(axis=2)
    mn = ln.reshape(H, V, 2).min(axis=2)
    z = f64(gs) * (mx * sigmoid(mn))
    s = 0.0625 * ((x_cand.T @ mxq(z, 0, "e4m3")))
    pa = s[np.arange(C)[:, None], runs(n2, C)]
    pb = s[np.arange(C)[:, None], runs(n3, C)]
    ra = np.maximum(pa, pb)
    out = s.copy()
    out[np.arange(C)[:, None], runs(n2, C)] = ra
    return out

@@ -1,0 +1,195 @@
+from contextlib import ExitStack
+
+import concourse.mybir as mybir
+
+K, T, S, V, H, C, W = 512, 2048, 1024, 512, 512, 512, 256
+FLOPS = 2 * K * H * S + 2 * K * C * V
+
+F32 = mybir.dt.float32
+BF16 = mybir.dt.bfloat16
+I32 = mybir.dt.int32
+U32 = mybir.dt.uint32
+U16 = mybir.dt.uint16
+U8 = mybir.dt.uint8
+FP8X4 = mybir.dt.float8_e4m3fn_x4
+ALU = mybir.AluOpType
+ACT = mybir.ActivationFunctionType
+
+P = 128
+PACK = 4
+BANK = 512
+HALVES = 2
+VH = V // HALVES
+
+
+def tile_picked_candpgatefill_none_p_kernel(tc, x_words, x_scales, w1, gs, offs, n1, cand, n2, n3, out):
+    nc = tc.nc
+    with ExitStack() as ctx:
+        keep = ctx.enter_context(tc.tile_pool(name="keep", bufs=1))
+        psum_y = ctx.enter_context(tc.psum_pool(name="psum_y", bufs=4))
+        psum_s = ctx.enter_context(tc.psum_pool(name="psum_s", bufs=1))
+
+        offs_t = keep.tile([P, S // 16], U16, name="offs_t")
+        cand_t = keep.tile([P, C // 16], U16, name="cand_t")
+        n1_t = keep.tile([P, S // 16], U16, name="n1_t")
+        n2_t = keep.tile([P, W // 16], U16, name="n2_t")
+        n3_t = keep.tile([P, W // 16], U16, name="n3_t")
+        xs = keep.tile([P, T], U8, name="xs", align_bytes=64)
+        xw = keep.tile([P, T], I32, name="xw", align_bytes=64)
+        w_raw = [keep.tile([P, PACK, H // 2], F32, name=f"w_raw{h}") for h in range(2)]
+        gs_t = keep.tile([P, PACK], F32, name="gs_t")
+
+        nc.vector.memset(xs[:].bitcast(I32), 0)
+        nc.sync.dma_start(offs_t[:], offs)
+        w_rows = w1.rearrange("(p j) c -> p j c", j=PACK)
+        for q in range(4):
+            nc.sync.dma_start(xs[32 * q : 32 * q + 4, :].bitcast(I32), x_scales[0, 4 * q : 4 * q + 4, :].bitcast(I32))
+        for h in range(2):
+            nc.sync.dma_start(w_raw[h][:], w_rows[:, :, h * (H // 2) : (h + 1) * (H // 2)])
+        nc.sync.dma_start(xw[:], x_words[0].rearrange("p n r -> p (n r)").bitcast(I32))
+        nc.sync.dma_start(cand_t[:], cand)
+        nc.sync.dma_start(n1_t[:], n1)
+        nc.sync.dma_start(gs_t[:], gs.rearrange("(p t) o -> p (t o)", t=PACK))
+        nc.sync.dma_start(n2_t[:], n2)
+        nc.sync.dma_start(n3_t[:], n3)
+
+        q_scales = keep.tile([P, S], U8, name="q_scales", align_bytes=64)
+        c_scales_l = keep.tile([P, C], U8, name="c_scales_l", align_bytes=64)
+        c_scales = keep.tile([P, C], U8, name="c_scales", align_bytes=64)
+        nc.vector.tensor_copy(q_scales[:], xs[:].indirect(offs_t[:]))
+        nc.vector.tensor_copy(c_scales_l[:], xs[:].indirect(cand_t[:]))
+
+        w_bf = keep.tile([P, PACK, P, PACK], BF16, name="w_bf", align_bytes=64)
+        for h in range(2):
+            nc.scalar.copy(
+                w_bf[:, :, h * 64 : (h + 1) * 64, :].rearrange("p t m j -> p m j t"),
+                w_raw[h][:].rearrange("p j (m t) -> p m j t", t=PACK),
+            )
+        w_words = keep.tile([P, H], U32, name="w_words", align_bytes=64)
+        w_scales = keep.tile([P, H], U8, name="w_scales", align_bytes=64)
+
+        q_words = [keep.tile([P, BANK], U32, name=f"q_words{h}", align_bytes=64) for h in range(2)]
+        nc.vector.tensor_copy(q_words[0][:], xw[:].bitcast(U32).indirect(offs_t[:, 0:32]))
+        nc.vector.tensor_copy(
+            c_scales[:].rearrange("p (t m) -> p t m", t=PACK), c_scales_l[:].rearrange("p (m t) -> p t m", t=PACK)
+        )
+        nc.vector.quantize_mx(out=w_words[:].bitcast(FP8X4), scales=w_scales[:], in_=w_bf[:].rearrange("p t m j -> p (t m j)"))
+        nc.vector.tensor_copy(q_words[1][:], xw[:].bitcast(U32).indirect(offs_t[:, 32:64]))
+        c_words_l = keep.tile([P, C], U32, name="c_words_l", align_bytes=64)
+        c_words = keep.tile([P, C], U32, name="c_words", align_bytes=64)
+        nc.vector.tensor_copy(c_words_l[:], xw[:].bitcast(U32).indirect(cand_t[:]))
+
+        y = [keep.tile([P, S], F32, name=f"y{t}") for t in range(PACK)]
+        for t in range(PACK):
+            for h in range(2):
+                acc = psum_y.tile([P, BANK], F32, name="acc_y")
+                nc.tensor.matmul_mx(
+                    out=acc[:],
+                    lhsT=w_words[:, t * P : (t + 1) * P].bitcast(FP8X4),
+                    lhsT_scale=w_scales[:, t * P : (t + 1) * P],
+                    rhs=q_words[h][:].bitcast(FP8X4),
+                    rhs_scale=q_scales[:, h * BANK : (h + 1) * BANK],
+                    start=True,
+                    stop=True,
+                )
+                nc.scalar.copy(y[t][:, h * BANK : (h + 1) * BANK], acc[:])
+
+        acc_s = [psum_s.tile([P, V], F32, name=f"acc_s{t}") for t in range(PACK)]
+        s = [keep.tile([P, V], F32, name=f"s{t}") for t in range(PACK)]
+        ln = [[keep.tile([P, VH, 2], F32, name=f"ln{h}{t}") for t in range(PACK)] for h in range(HALVES)]
+        mn = [[keep.tile([P, VH], F32, name=f"mn{h}{t}") for t in range(PACK)] for h in range(HALVES)]
+        sg = [[keep.tile([P, VH], F32, name=f"sg{h}{t}") for t in range(PACK)] for h in range(HALVES)]
+        mx = [keep.tile([P, PACK, VH], F32, name=f"mx{h}") for h in range(HALVES)]
+        gate = [keep.tile([P, PACK, VH], F32, name=f"gate{h}") for h in range(HALVES)]
+        z_bf = [keep.tile([P, VH, PACK], BF16, name=f"z_bf{h}", align_bytes=64) for h in range(HALVES)]
+        z_words = [keep.tile([P, VH], U32, name=f"z_words{h}", align_bytes=64) for h in range(HALVES)]
+        z_scales = [keep.tile([P, VH], U8, name=f"z_scales{h}", align_bytes=64) for h in range(HALVES)]
+
+        def line_up(h, t):
+            nc.vector.tensor_copy(ln[h][t][:].rearrange("p v e -> p (v e)"), y[t][:].indirect(n1_t[:, 32 * h : 32 * (h + 1)]))
+
+        def smaller(h, t):
+            nc.vector.tensor_tensor(mn[h][t][:], ln[h][t][:, :, 0], ln[h][t][:, :, 1], ALU.min)
+            nc.scalar.activation(sg[h][t][:], mn[h][t][:], ACT.Sigmoid)
+            nc.scalar.activation(gate[h][:, t, :], sg[h][t][:], ACT.Copy, scale=gs_t[:, t : t + 1])
+
+        def larger(h, t):
+            nc.vector.tensor_tensor(mx[h][:, t, :], ln[h][t][:, :, 0], ln[h][t][:, :, 1], ALU.max)
+
+        def product(h):
+            nc.vector.tensor_tensor(
+                z_bf[h][:].rearrange("p (c i) t -> p c t i", i=2),
+                mx[h][:].rearrange("p t (c i) -> p c t i", i=2),
+                gate[h][:].rearrange("p t (c i) -> p c t i", i=2),
+                ALU.mult,
+            )
+
+        def score(h):
+            nc.vector.quantize_mx(out=z_words[h][:].bitcast(FP8X4), scales=z_scales[h][:], in_=z_bf[h][:].rearrange("p v t -> p (v t)"))
+            for t in range(PACK):
+                nc.tensor.matmul_mx(
+                    out=acc_s[t][:, h * VH : (h + 1) * VH],
+                    lhsT=c_words[:, t * P : (t + 1) * P].bitcast(FP8X4),
+                    lhsT_scale=c_scales[:, t * P : (t + 1) * P],
+                    rhs=z_words[h][:].bitcast(FP8X4),
+                    rhs_scale=z_scales[h][:],
+                    start=True,
+                    stop=True,
+                )
+                nc.scalar.activation(s[t][:, h * VH : (h + 1) * VH], acc_s[t][:, h * VH : (h + 1) * VH], ACT.Copy, scale=0.0625)
+
+        line_up(0, 0)
+        nc.vector.tensor_copy(
+            c_words[:].rearrange("p (t m) -> p m t", t=PACK), c_words_l[:].rearrange("p (m t) -> p m t", t=PACK)
+        )
+        for t in range(PACK):
+            if t + 1 < PACK:
+                line_up(0, t + 1)
+            else:
+                line_up(1, 0)
+            smaller(0, t)
+            larger(0, t)
+        line_up(1, 1)
+        product(0)
+        smaller(1, 0)
+        score(0)
+        line_up(1, 2)
+        smaller(1, 1)
+        line_up(1, 3)
+        smaller(1, 2)
+        larger(1, 0)
+        smaller(1, 3)
+        larger(1, 1)
+        larger(1, 2)
+        larger(1, 3)
+        product(1)
+        score(1)
+
+        pa = [keep.tile([P, W], F32, name=f"pa{t}") for t in range(PACK)]
+        gap = [keep.tile([P, W], F32, name=f"gap{t}") for t in range(PACK)]
+        lift = [keep.tile([P, W], F32, name=f"lift{t}") for t in range(PACK)]
+        out_rows = out.rearrange("(p t) v -> p t v", t=PACK)
+
+        def fetch_a(t):
+            nc.vector.tensor_copy(pa[t][:], s[t][:].indirect(n2_t[:]))
+
+        def fetch_gap(t):
+            nc.vector.tensor_tensor(gap[t][:], s[t][:].indirect(n3_t[:]), pa[t][:], ALU.subtract)
+            nc.scalar.activation(lift[t][:], gap[t][:], ACT.Relu)
+
+        def put(t):
+            nc.vector.tensor_tensor(s[t][:].indirect(n2_t[:]), pa[t][:], lift[t][:], ALU.add)
+            nc.sync.dma_start(out_rows[:, t, :], s[t][:])
+
+        fetch_a(0)
+        fetch_a(1)
+        fetch_gap(0)
+        fetch_gap(1)
+        fetch_a(2)
+        put(0)
+        fetch_gap(2)
+        fetch_a(3)
+        put(1)
+        fetch_gap(3)
+        put(2)
+        put(3)

@@ -40,13 +40,15 @@ def tile_picked_candpgatefill_none_p_kernel(tc, x_words, x_scales, w1, gs, offs,
         gs_t = keep.tile([P, PACK], F32, name="gs_t")
 
         nc.vector.memset(xs[:].bitcast(I32), 0)
-        nc.sync.dma_start(offs_t[:], offs)
+        x_rows = x_words[0].rearrange("p n r -> p (n r)").bitcast(I32)
         w_rows = w1.rearrange("(p j) c -> p j c", j=PACK)
+        nc.sync.dma_start(offs_t[:], offs)
+        nc.sync.dma_start(xw[:, 0 : T // 2], x_rows[:, 0 : T // 2])
         for q in range(4):
-            nc.sync.dma_start(xs[32 * q : 32 * q + 4, :].bitcast(I32), x_scales[0, 4 * q : 4 * q + 4, :].bitcast(I32))
+            (nc.sync if q < 2 else nc.scalar).dma_start(xs[32 * q : 32 * q + 4, :].bitcast(I32), x_scales[0, 4 * q : 4 * q + 4, :].bitcast(I32))
+        nc.sync.dma_start(xw[:, T // 2 : T], x_rows[:, T // 2 : T])
         for h in range(2):
             nc.sync.dma_start(w_raw[h][:], w_rows[:, :, h * (H // 2) : (h + 1) * (H // 2)])
-        nc.sync.dma_start(xw[:], x_words[0].rearrange("p n r -> p (n r)").bitcast(I32))
         nc.sync.dma_start(cand_t[:], cand)
         nc.sync.dma_start(n1_t[:], n1)
         nc.sync.dma_start(gs_t[:], gs.rearrange("(p t) o -> p (t o)", t=PACK))
@@ -54,30 +56,36 @@ def tile_picked_candpgatefill_none_p_kernel(tc, x_words, x_scales, w1, gs, offs,
         nc.sync.dma_start(n3_t[:], n3)
 
         q_scales = keep.tile([P, S], U8, name="q_scales", align_bytes=64)
-        c_scales_l = keep.tile([P, C], U8, name="c_scales_l", align_bytes=64)
-        c_scales = keep.tile([P, C], U8, name="c_scales", align_bytes=64)
+        q_words = keep.tile([P, S], U32, name="q_words", align_bytes=64)
         nc.vector.tensor_copy(q_scales[:], xs[:].indirect(offs_t[:]))
-        nc.vector.tensor_copy(c_scales_l[:], xs[:].indirect(cand_t[:]))
+        nc.vector.tensor_copy(q_words[:], xw[:].bitcast(U32).indirect(offs_t[:]))
 
-        w_bf = keep.tile([P, PACK, P, PACK], BF16, name="w_bf", align_bytes=64)
+        w_bf = [keep.tile([P, 2, P, PACK], BF16, name=f"w_bf{u}", tag=f"w_bf{u}", align_bytes=64) for u in range(2)]
         for h in range(2):
-            nc.scalar.copy(
-                w_bf[:, :, h * 64 : (h + 1) * 64, :].rearrange("p t m j -> p m j t"),
-                w_raw[h][:].rearrange("p j (m t) -> p m j t", t=PACK),
-            )
+            for u in range(2):
+                nc.scalar.copy(
+                    w_bf[u][:, :, 64 * h : 64 * (h + 1), :].rearrange("p t m j -> p m j t"),
+                    w_raw[h][:].rearrange("p j (m t) -> p m j t", t=PACK)[:, :, :, 2 * u : 2 * u + 2],
+                )
         w_words = keep.tile([P, H], U32, name="w_words", align_bytes=64)
         w_scales = keep.tile([P, H], U8, name="w_scales", align_bytes=64)
 
-        q_words = [keep.tile([P, BANK], U32, name=f"q_words{h}", align_bytes=64) for h in range(2)]
-        nc.vector.tensor_copy(q_words[0][:], xw[:].bitcast(U32).indirect(offs_t[:, 0:32]))
-        nc.vector.tensor_copy(
-            c_scales[:].rearrange("p (t m) -> p t m", t=PACK), c_scales_l[:].rearrange("p (m t) -> p t m", t=PACK)
-        )
-        nc.vector.quantize_mx(out=w_words[:].bitcast(FP8X4), scales=w_scales[:], in_=w_bf[:].rearrange("p t m j -> p (t m j)"))
-        nc.vector.tensor_copy(q_words[1][:], xw[:].bitcast(U32).indirect(offs_t[:, 32:64]))
-        c_words_l = keep.tile([P, C], U32, name="c_words_l", align_bytes=64)
-        c_words = keep.tile([P, C], U32, name="c_words", align_bytes=64)
+        def pack_weights(u):
+            nc.vector.quantize_mx(
+                out=w_words[:, 2 * u * P : 2 * (u + 1) * P].bitcast(FP8X4),
+                scales=w_scales[:, 2 * u * P : 2 * (u + 1) * P],
+                in_=w_bf[u][:].rearrange("p t m j -> p (t m j)"),
+            )
+
+        pack_weights(0)
+        c_scales_l = keep.tile([P, C], U8, name="c_scales_l", tag="w_bf0", align_bytes=64)
+        nc.vector.tensor_copy(c_scales_l[:], xs[:].indirect(cand_t[:]))
+        pack_weights(1)
+        c_words_l = keep.tile([P, C], U32, name="c_words_l", tag="w_bf1", align_bytes=64)
         nc.vector.tensor_copy(c_words_l[:], xw[:].bitcast(U32).indirect(cand_t[:]))
+        c_scales = [keep.tile([P, 2, P], U8, name="c_scales0", align_bytes=64)]
+        c_words = [keep.tile([P, 2, P], U32, name="c_words0", align_bytes=64)]
+        nc.vector.tensor_copy(c_scales[0][:], c_scales_l[:].rearrange("p (m t) -> p t m", t=PACK)[:, 0:2, :])
 
         y = [keep.tile([P, S], F32, name=f"y{t}") for t in range(PACK)]
         for t in range(PACK):
@@ -87,7 +95,7 @@ def tile_picked_candpgatefill_none_p_kernel(tc, x_words, x_scales, w1, gs, offs,
                     out=acc[:],
                     lhsT=w_words[:, t * P : (t + 1) * P].bitcast(FP8X4),
                     lhsT_scale=w_scales[:, t * P : (t + 1) * P],
-                    rhs=q_words[h][:].bitcast(FP8X4),
+                    rhs=q_words[:, h * BANK : (h + 1) * BANK].bitcast(FP8X4),
                     rhs_scale=q_scales[:, h * BANK : (h + 1) * BANK],
                     start=True,
                     stop=True,
@@ -95,15 +103,17 @@ def tile_picked_candpgatefill_none_p_kernel(tc, x_words, x_scales, w1, gs, offs,
                 nc.scalar.copy(y[t][:, h * BANK : (h + 1) * BANK], acc[:])
 
         acc_s = [psum_s.tile([P, V], F32, name=f"acc_s{t}") for t in range(PACK)]
+        acc_late = [psum_y.tile([P, BANK], F32, name="acc_y") for t in range(3)]
         s = [keep.tile([P, V], F32, name=f"s{t}") for t in range(PACK)]
         ln = [[keep.tile([P, VH, 2], F32, name=f"ln{h}{t}") for t in range(PACK)] for h in range(HALVES)]
         mn = [[keep.tile([P, VH], F32, name=f"mn{h}{t}") for t in range(PACK)] for h in range(HALVES)]
         sg = [[keep.tile([P, VH], F32, name=f"sg{h}{t}") for t in range(PACK)] for h in range(HALVES)]
         mx = [keep.tile([P, PACK, VH], F32, name=f"mx{h}") for h in range(HALVES)]
         gate = [keep.tile([P, PACK, VH], F32, name=f"gate{h}") for h in range(HALVES)]
-        z_bf = [keep.tile([P, VH, PACK], BF16, name=f"z_bf{h}", align_bytes=64) for h in range(HALVES)]
-        z_words = [keep.tile([P, VH], U32, name=f"z_words{h}", align_bytes=64) for h in range(HALVES)]
-        z_scales = [keep.tile([P, VH], U8, name=f"z_scales{h}", align_bytes=64) for h in range(HALVES)]
+        pieces = [(0, 256), (256, 384), (384, 512)]
+        z_bf = [keep.tile([P, b - a, PACK], BF16, name=f"z_bf{a}", tag=f"z_bf{a}", align_bytes=64) for a, b in pieces]
+        z_words = [keep.tile([P, b - a], U32, name=f"z_words{a}", align_bytes=64) for a, b in pieces]
+        z_scales = [keep.tile([P, b - a], U8, name=f"z_scales{a}", align_bytes=64) for a, b in pieces]
 
         def line_up(h, t):
             nc.vector.tensor_copy(ln[h][t][:].rearrange("p v e -> p (v e)"), y[t][:].indirect(n1_t[:, 32 * h : 32 * (h + 1)]))
@@ -116,32 +126,36 @@ def tile_picked_candpgatefill_none_p_kernel(tc, x_words, x_scales, w1, gs, offs,
         def larger(h, t):
             nc.vector.tensor_tensor(mx[h][:, t, :], ln[h][t][:, :, 0], ln[h][t][:, :, 1], ALU.max)
 
-        def product(h):
+        def product(k):
+            a, b = pieces[k]
+            h = a // VH
             nc.vector.tensor_tensor(
-                z_bf[h][:].rearrange("p (c i) t -> p c t i", i=2),
-                mx[h][:].rearrange("p t (c i) -> p c t i", i=2),
-                gate[h][:].rearrange("p t (c i) -> p c t i", i=2),
+                z_bf[k][:].rearrange("p (c i) t -> p c t i", i=2),
+                mx[h][:, :, a - h * VH : b - h * VH].rearrange("p t (c i) -> p c t i", i=2),
+                gate[h][:, :, a - h * VH : b - h * VH].rearrange("p t (c i) -> p c t i", i=2),
                 ALU.mult,
             )
 
-        def score(h):
-            nc.vector.quantize_mx(out=z_words[h][:].bitcast(FP8X4), scales=z_scales[h][:], in_=z_bf[h][:].rearrange("p v t -> p (v t)"))
-            for t in range(PACK):
-                nc.tensor.matmul_mx(
-                    out=acc_s[t][:, h * VH : (h + 1) * VH],
-                    lhsT=c_words[:, t * P : (t + 1) * P].bitcast(FP8X4),
-                    lhsT_scale=c_scales[:, t * P : (t + 1) * P],
-                    rhs=z_words[h][:].bitcast(FP8X4),
-                    rhs_scale=z_scales[h][:],
-                    start=True,
-                    stop=True,
-                )
-                nc.scalar.activation(s[t][:, h * VH : (h + 1) * VH], acc_s[t][:, h * VH : (h + 1) * VH], ACT.Copy, scale=0.0625)
+        def pack(k):
+            nc.vector.quantize_mx(out=z_words[k][:].bitcast(FP8X4), scales=z_scales[k][:], in_=z_bf[k][:].rearrange("p v t -> p (v t)"))
+
+        def score(t, k, acc):
+            a, b = pieces[k]
+            nc.tensor.matmul_mx(
+                out=acc[:, a:b],
+                lhsT=c_words[t // 2][:, t % 2, :].bitcast(FP8X4),
+                lhsT_scale=c_scales[t // 2][:, t % 2, :],
+                rhs=z_words[k][:].bitcast(FP8X4),
+                rhs_scale=z_scales[k][:],
+                start=True,
+                stop=True,
+            )
+
+        def leave(t, a, b, acc):
+            nc.scalar.activation(s[t][:, a:b], acc[:, a:b], ACT.Copy, scale=0.0625)
 
         line_up(0, 0)
-        nc.vector.tensor_copy(
-            c_words[:].rearrange("p (t m) -> p m t", t=PACK), c_words_l[:].rearrange("p (m t) -> p m t", t=PACK)
-        )
+        nc.vector.tensor_copy(c_words[0][:].rearrange("p t m -> p m t"), c_words_l[:].rearrange("p (m t) -> p m t", t=PACK)[:, :, 0:2])
         for t in range(PACK):
             if t + 1 < PACK:
                 line_up(0, t + 1)
@@ -152,7 +166,10 @@ def tile_picked_candpgatefill_none_p_kernel(tc, x_words, x_scales, w1, gs, offs,
         line_up(1, 1)
         product(0)
         smaller(1, 0)
-        score(0)
+        pack(0)
+        for t in range(2):
+            score(t, 0, acc_s[t])
+            leave(t, 0, VH, acc_s[t])
         line_up(1, 2)
         smaller(1, 1)
         line_up(1, 3)
@@ -163,7 +180,25 @@ def tile_picked_candpgatefill_none_p_kernel(tc, x_words, x_scales, w1, gs, offs,
         larger(1, 2)
         larger(1, 3)
         product(1)
-        score(1)
+        product(2)
+        pack(1)
+        pack(2)
+        score(0, 1, acc_late[0])
+        leave(0, *pieces[1], acc_late[0])
+        score(0, 2, acc_late[1])
+        score(1, 1, acc_late[2])
+        score(1, 2, acc_late[2])
+        leave(1, VH, V, acc_late[2])
+        c_scales.append(keep.tile([P, 2, P], U8, name="c_scales1", tag="z_bf256", align_bytes=64))
+        c_words.append(keep.tile([P, 2, P], U32, name="c_words1", tag="z_bf384", align_bytes=64))
+        nc.vector.tensor_copy(c_scales[1][:], c_scales_l[:].rearrange("p (m t) -> p t m", t=PACK)[:, 2:4, :])
+        nc.vector.tensor_copy(c_words[1][:].rearrange("p t m -> p m t"), c_words_l[:].rearrange("p (m t) -> p m t", t=PACK)[:, :, 2:4])
+        a, b = pieces[2]
+        nc.vector.tensor_scalar(s[0][:, a:b], acc_late[1][:, a:b], 0.0625, None, ALU.mult)
+        for t in range(2, PACK):
+            for k in range(3):
+                score(t, k, acc_s[t])
+            leave(t, 0, V, acc_s[t])
 
         pa = [keep.tile([P, W], F32, name=f"pa{t}") for t in range(PACK)]
         gap = [keep.tile([P, W], F32, name=f"gap{t}") for t in range(PACK)]

@@ -45,7 +45,7 @@ def tile_picked_candpgatefill_none_p_kernel(tc, x_words, x_scales, w1, gs, offs,
         nc.sync.dma_start(offs_t[:], offs)
         nc.sync.dma_start(xw[:, 0 : T // 2], x_rows[:, 0 : T // 2])
         for q in range(4):
-            (nc.sync if q < 2 else nc.scalar).dma_start(xs[32 * q : 32 * q + 4, :].bitcast(I32), x_scales[0, 4 * q : 4 * q + 4, :].bitcast(I32))
+            nc.sync.dma_start(xs[32 * q : 32 * q + 4, :].bitcast(I32), x_scales[0, 4 * q : 4 * q + 4, :].bitcast(I32))
         nc.sync.dma_start(xw[:, T // 2 : T], x_rows[:, T // 2 : T])
         for h in range(2):
             nc.sync.dma_start(w_raw[h][:], w_rows[:, :, h * (H // 2) : (h + 1) * (H // 2)])

from contextlib import ExitStack

import concourse.mybir as mybir

K, T, S, V, H, C, W = 512, 2048, 1024, 512, 512, 512, 256
FLOPS = 2 * K * H * S + 2 * K * C * V

F32 = mybir.dt.float32
BF16 = mybir.dt.bfloat16
I32 = mybir.dt.int32
U32 = mybir.dt.uint32
U16 = mybir.dt.uint16
U8 = mybir.dt.uint8
FP8X4 = mybir.dt.float8_e4m3fn_x4
ALU = mybir.AluOpType
ACT = mybir.ActivationFunctionType

P = 128
PACK = 4
BANK = 512
HALVES = 2
VH = V // HALVES


def tile_picked_candpgatefill_none_p_kernel(tc, x_words, x_scales, w1, gs, offs, n1, cand, n2, n3, out):
    nc = tc.nc
    with ExitStack() as ctx:
        keep = ctx.enter_context(tc.tile_pool(name="keep", bufs=1))
        psum_y = ctx.enter_context(tc.psum_pool(name="psum_y", bufs=4))
        psum_s = ctx.enter_context(tc.psum_pool(name="psum_s", bufs=1))

        offs_t = keep.tile([P, S // 16], U16, name="offs_t")
        cand_t = keep.tile([P, C // 16], U16, name="cand_t")
        n1_t = keep.tile([P, S // 16], U16, name="n1_t")
        n2_t = keep.tile([P, W // 16], U16, name="n2_t")
        n3_t = keep.tile([P, W // 16], U16, name="n3_t")
        xs = keep.tile([P, T], U8, name="xs", align_bytes=64)
        xw = keep.tile([P, T], I32, name="xw", align_bytes=64)
        w_raw = [keep.tile([P, PACK, H // 2], F32, name=f"w_raw{h}") for h in range(2)]
        gs_t = keep.tile([P, PACK], F32, name="gs_t")

        nc.vector.memset(xs[:].bitcast(I32), 0)
        x_rows = x_words[0].rearrange("p n r -> p (n r)").bitcast(I32)
        w_rows = w1.rearrange("(p j) c -> p j c", j=PACK)
        nc.sync.dma_start(offs_t[:], offs)
        nc.sync.dma_start(xw[:, 0 : T // 2], x_rows[:, 0 : T // 2])
        for q in range(4):
            nc.sync.dma_start(xs[32 * q : 32 * q + 4, :].bitcast(I32), x_scales[0, 4 * q : 4 * q + 4, :].bitcast(I32))
        nc.sync.dma_start(xw[:, T // 2 : T], x_rows[:, T // 2 : T])
        for h in range(2):
            nc.sync.dma_start(w_raw[h][:], w_rows[:, :, h * (H // 2) : (h + 1) * (H // 2)])
        nc.sync.dma_start(cand_t[:], cand)
        nc.sync.dma_start(n1_t[:], n1)
        nc.sync.dma_start(gs_t[:], gs.rearrange("(p t) o -> p (t o)", t=PACK))
        nc.sync.dma_start(n2_t[:], n2)
        nc.sync.dma_start(n3_t[:], n3)

        q_scales = keep.tile([P, S], U8, name="q_scales", align_bytes=64)
        q_words = keep.tile([P, S], U32, name="q_words", align_bytes=64)
        nc.vector.tensor_copy(q_scales[:], xs[:].indirect(offs_t[:]))
        nc.vector.tensor_copy(q_words[:], xw[:].bitcast(U32).indirect(offs_t[:]))

        w_bf = [keep.tile([P, 2, P, PACK], BF16, name=f"w_bf{u}", tag=f"w_bf{u}", align_bytes=64) for u in range(2)]
        for h in range(2):
            for u in range(2):
                nc.scalar.copy(
                    w_bf[u][:, :, 64 * h : 64 * (h + 1), :].rearrange("p t m j -> p m j t"),
                    w_raw[h][:].rearrange("p j (m t) -> p m j t", t=PACK)[:, :, :, 2 * u : 2 * u + 2],
                )
        w_words = keep.tile([P, H], U32, name="w_words", align_bytes=64)
        w_scales = keep.tile([P, H], U8, name="w_scales", align_bytes=64)

        def pack_weights(u):
            nc.vector.quantize_mx(
                out=w_words[:, 2 * u * P : 2 * (u + 1) * P].bitcast(FP8X4),
                scales=w_scales[:, 2 * u * P : 2 * (u + 1) * P],
                in_=w_bf[u][:].rearrange("p t m j -> p (t m j)"),
            )

        pack_weights(0)
        c_scales_l = keep.tile([P, C], U8, name="c_scales_l", tag="w_bf0", align_bytes=64)
        nc.vector.tensor_copy(c_scales_l[:], xs[:].indirect(cand_t[:]))
        pack_weights(1)
        c_words_l = keep.tile([P, C], U32, name="c_words_l", tag="w_bf1", align_bytes=64)
        nc.vector.tensor_copy(c_words_l[:], xw[:].bitcast(U32).indirect(cand_t[:]))
        c_scales = [keep.tile([P, 2, P], U8, name="c_scales0", align_bytes=64)]
        c_words = [keep.tile([P, 2, P], U32, name="c_words0", align_bytes=64)]
        nc.vector.tensor_copy(c_scales[0][:], c_scales_l[:].rearrange("p (m t) -> p t m", t=PACK)[:, 0:2, :])

        y = [keep.tile([P, S], F32, name=f"y{t}") for t in range(PACK)]
        for t in range(PACK):
            for h in range(2):
                acc = psum_y.tile([P, BANK], F32, name="acc_y")
                nc.tensor.matmul_mx(
                    out=acc[:],
                    lhsT=w_words[:, t * P : (t + 1) * P].bitcast(FP8X4),
                    lhsT_scale=w_scales[:, t * P : (t + 1) * P],
                    rhs=q_words[:, h * BANK : (h + 1) * BANK].bitcast(FP8X4),
                    rhs_scale=q_scales[:, h * BANK : (h + 1) * BANK],
                    start=True,
                    stop=True,
                )
                nc.scalar.copy(y[t][:, h * BANK : (h + 1) * BANK], acc[:])

        acc_s = [psum_s.tile([P, V], F32, name=f"acc_s{t}") for t in range(PACK)]
        acc_late = [psum_y.tile([P, BANK], F32, name="acc_y") for t in range(3)]
        s = [keep.tile([P, V], F32, name=f"s{t}") for t in range(PACK)]
        ln = [[keep.tile([P, VH, 2], F32, name=f"ln{h}{t}") for t in range(PACK)] for h in range(HALVES)]
        mn = [[keep.tile([P, VH], F32, name=f"mn{h}{t}") for t in range(PACK)] for h in range(HALVES)]
        sg = [[keep.tile([P, VH], F32, name=f"sg{h}{t}") for t in range(PACK)] for h in range(HALVES)]
        mx = [keep.tile([P, PACK, VH], F32, name=f"mx{h}") for h in range(HALVES)]
        gate = [keep.tile([P, PACK, VH], F32, name=f"gate{h}") for h in range(HALVES)]
        pieces = [(0, 256), (256, 384), (384, 512)]
        z_bf = [keep.tile([P, b - a, PACK], BF16, name=f"z_bf{a}", tag=f"z_bf{a}", align_bytes=64) for a, b in pieces]
        z_words = [keep.tile([P, b - a], U32, name=f"z_words{a}", align_bytes=64) for a, b in pieces]
        z_scales = [keep.tile([P, b - a], U8, name=f"z_scales{a}", align_bytes=64) for a, b in pieces]

        def line_up(h, t):
            nc.vector.tensor_copy(ln[h][t][:].rearrange("p v e -> p (v e)"), y[t][:].indirect(n1_t[:, 32 * h : 32 * (h + 1)]))

        def smaller(h, t):
            nc.vector.tensor_tensor(mn[h][t][:], ln[h][t][:, :, 0], ln[h][t][:, :, 1], ALU.min)
            nc.scalar.activation(sg[h][t][:], mn[h][t][:], ACT.Sigmoid)
            nc.scalar.activation(gate[h][:, t, :], sg[h][t][:], ACT.Copy, scale=gs_t[:, t : t + 1])

        def larger(h, t):
            nc.vector.tensor_tensor(mx[h][:, t, :], ln[h][t][:, :, 0], ln[h][t][:, :, 1], ALU.max)

        def product(k):
            a, b = pieces[k]
            h = a // VH
            nc.vector.tensor_tensor(
                z_bf[k][:].rearrange("p (c i) t -> p c t i", i=2),
                mx[h][:, :, a - h * VH : b - h * VH].rearrange("p t (c i) -> p c t i", i=2),
                gate[h][:, :, a - h * VH : b - h * VH].rearrange("p t (c i) -> p c t i", i=2),
                ALU.mult,
            )

        def pack(k):
            nc.vector.quantize_mx(out=z_words[k][:].bitcast(FP8X4), scales=z_scales[k][:], in_=z_bf[k][:].rearrange("p v t -> p (v t)"))

        def score(t, k, acc):
            a, b = pieces[k]
            nc.tensor.matmul_mx(
                out=acc[:, a:b],
                lhsT=c_words[t // 2][:, t % 2, :].bitcast(FP8X4),
                lhsT_scale=c_scales[t // 2][:, t % 2, :],
                rhs=z_words[k][:].bitcast(FP8X4),
                rhs_scale=z_scales[k][:],
                start=True,
                stop=True,
            )

        def leave(t, a, b, acc):
            nc.scalar.activation(s[t][:, a:b], acc[:, a:b], ACT.Copy, scale=0.0625)

        line_up(0, 0)
        nc.vector.tensor_copy(c_words[0][:].rearrange("p t m -> p m t"), c_words_l[:].rearrange("p (m t) -> p m t", t=PACK)[:, :, 0:2])
        for t in range(PACK):
            if t + 1 < PACK:
                line_up(0, t + 1)
            else:
                line_up(1, 0)
            smaller(0, t)
            larger(0, t)
        line_up(1, 1)
        product(0)
        smaller(1, 0)
        pack(0)
        for t in range(2):
            score(t, 0, acc_s[t])
            leave(t, 0, VH, acc_s[t])
        line_up(1, 2)
        smaller(1, 1)
        line_up(1, 3)
        smaller(1, 2)
        larger(1, 0)
        smaller(1, 3)
        larger(1, 1)
        larger(1, 2)
        larger(1, 3)
        product(1)
        product(2)
        pack(1)
        pack(2)
        score(0, 1, acc_late[0])
        leave(0, *pieces[1], acc_late[0])
        score(0, 2, acc_late[1])
        score(1, 1, acc_late[2])
        score(1, 2, acc_late[2])
        leave(1, VH, V, acc_late[2])
        c_scales.append(keep.tile([P, 2, P], U8, name="c_scales1", tag="z_bf256", align_bytes=64))
        c_words.append(keep.tile([P, 2, P], U32, name="c_words1", tag="z_bf384", align_bytes=64))
        nc.vector.tensor_copy(c_scales[1][:], c_scales_l[:].rearrange("p (m t) -> p t m", t=PACK)[:, 2:4, :])
        nc.vector.tensor_copy(c_words[1][:].rearrange("p t m -> p m t"), c_words_l[:].rearrange("p (m t) -> p m t", t=PACK)[:, :, 2:4])
        a, b = pieces[2]
        nc.vector.tensor_scalar(s[0][:, a:b], acc_late[1][:, a:b], 0.0625, None, ALU.mult)
        for t in range(2, PACK):
            for k in range(3):
                score(t, k, acc_s[t])
            leave(t, 0, V, acc_s[t])

        pa = [keep.tile([P, W], F32, name=f"pa{t}") for t in range(PACK)]
        gap = [keep.tile([P, W], F32, name=f"gap{t}") for t in range(PACK)]
        lift = [keep.tile([P, W], F32, name=f"lift{t}") for t in range(PACK)]
        out_rows = out.rearrange("(p t) v -> p t v", t=PACK)

        def fetch_a(t):
            nc.vector.tensor_copy(pa[t][:], s[t][:].indirect(n2_t[:]))

        def fetch_gap(t):
            nc.vector.tensor_tensor(gap[t][:], s[t][:].indirect(n3_t[:]), pa[t][:], ALU.subtract)
            nc.scalar.activation(lift[t][:], gap[t][:], ACT.Relu)

        def put(t):
            nc.vector.tensor_tensor(s[t][:].indirect(n2_t[:]), pa[t][:], lift[t][:], ALU.add)
            nc.sync.dma_start(out_rows[:, t, :], s[t][:])

        fetch_a(0)
        fetch_a(1)
        fetch_gap(0)
        fetch_gap(1)
        fetch_a(2)
        put(0)
        fetch_gap(2)
        fetch_a(3)
        put(1)
        fetch_gap(3)
        put(2)
        put(3)
